import numpy as np
import ml_dtypes


def mxq(x, axis, fmt="e4m3"):
    dtype, down = {"e4m3": (ml_dtypes.float8_e4m3fn, 7), "e5m2": (ml_dtypes.float8_e5m2, 14)}[fmt]
    v = np.moveaxis(np.asarray(x, np.float32).astype(ml_dtypes.bfloat16).astype(np.float64), axis, -1)
    blocks = v.reshape(v.shape[:-1] + (-1, 32))
    amax = np.abs(blocks).max(-1, keepdims=True)
    byte = np.maximum(np.where(amax > 0, np.frexp(amax)[1] - 1 + 127, 0) - down, 1)
    scale = np.exp2(byte - 127.0)
    codes = (blocks / scale).astype(np.float32).astype(dtype).astype(np.float64)
    return np.moveaxis((codes * scale).reshape(v.shape), -1, axis)


WIDE = False


def mx_kscale(k):
    if not WIDE:
        return np.ones(k)
    levels = np.array([10, -10, 5, -5, 0])
    if k % 512:
        return np.exp2(np.random.permutation(np.resize(levels, k // 32))).repeat(32)
    a = np.empty((k // 512, 16))
    for p in range(k // 512):
        a[p, :8] = np.random.permutation(np.resize(levels, 8))
        for g in range(8):
            far = levels[np.abs(levels - a[p, g]) >= 10]
            a[p, g + 8] = far[np.random.randint(len(far))]
    return np.exp2(a.ravel()).repeat(32)


def f64(x):
    return np.asarray(x).astype(np.float64)


def striped(idx):
    return np.tile(np.asarray(idx).reshape(-1, 16).T, (8, 1)).astype(np.uint16)


def unstriped(offs):
    return offs[:16].T.reshape(-1).astype(np.int64)


E2M1 = np.array([0.0, 0.5, 1.0, 1.5, 2.0, 3.0, 4.0, 6.0, -0.0, -0.5, -1.0, -1.5, -2.0, -3.0, -4.0, -6.0])


def pack_weight(w, fmt):
    k, n = w.shape
    w = f64(np.asarray(w, np.float32).astype(ml_dtypes.bfloat16)).reshape(k // 32, 32, n)
    amax = np.abs(w).max(1)
    if fmt == "e4m3":
        byte = np.frexp(amax)[1] - 1 + 127 - 7
    else:
        mant, ex = np.frexp(amax / 6.0)
        byte = np.where(mant > 0.5, ex, ex - 1) + 127
    byte = np.clip(np.where(amax > 0, byte, 1), 1, 254)
    scaled = (w * np.exp2(127.0 - byte)[:, None, :]).reshape(k, n).astype(np.float32)
    by_word = np.ascontiguousarray(scaled.reshape(k // 512, 128, 4, n).transpose(0, 1, 3, 2))
    if fmt == "e4m3":
        words = by_word.astype(ml_dtypes.float8_e4m3fn).view(np.uint8)
    else:
        c = by_word.astype(ml_dtypes.float4_e2m1fn).view(np.uint8) & 0xF
        words = (c[..., 0::2] | (c[..., 1::2] << 4)).reshape(k // 512, 128, 2 * n)
    return np.ascontiguousarray(words), np.ascontiguousarray(byte.astype(np.uint8).reshape(k // 512, 16, n))


def unpack_weight(words, scales, fmt):
    g, _, n = scales.shape
    words = np.ascontiguousarray(words).reshape(g, 128, n, -1)
    if fmt == "e4m3":
        vals = words.view(ml_dtypes.float8_e4m3fn).astype(np.float64)
    else:
        nib = np.empty((g, 128, n, 4), np.uint8)
        nib[..., 0::2] = words & 0xF
        nib[..., 1::2] = words >> 4
        vals = E2M1[nib]
    vals = vals * np.repeat(np.exp2(scales.astype(np.float64) - 127.0), 8, axis=1)[..., None]
    return vals.transpose(0, 1, 3, 2).reshape(g * 512, n)


def softplus(v):
    return np.log(1.0 + np.exp(v))


def sigmoid(v):
    return 1.0 / (1.0 + np.exp(-v))


def bf(x):
    return np.asarray(x, np.float32).astype(ml_dtypes.bfloat16)


def planes(Y):
    r, m = Y.shape
    b = f64(bf(Y)).reshape(r // 32, 32, m)
    amax = np.abs(b).max(1)
    byte = np.clip(np.where(amax > 0, np.frexp(amax)[1] - 1 + 127 - 7, 1), 1, 254)
    codes = (b * np.exp2(127.0 - byte)[:, None, :]).reshape(r, m).astype(np.float32).astype(ml_dtypes.float8_e4m3fn).view(np.uint8)
    words = codes.reshape(r // 512, 128, 4, m).transpose(0, 1, 3, 2)
    return np.ascontiguousarray(words), np.ascontiguousarray(byte.astype(np.uint8).reshape(r // 512, 16, m))


K, R, F, T, J, M = 512, 512, 512, 2048, 512, 256


def setup_inputs():
    n = np.random.standard_normal
    idx = np.random.permutation(T)[:J]
    idx2 = np.random.permutation(J)[:M]
    idx3 = np.random.permutation(J)[:M]
    fk = mx_kscale(K)
    fr = mx_kscale(R)
    tabp = pack_weight(n((K, T)) / fk[:, None], "e2m1")
    return {
        "tab_words": tabp[0],
        "tab_scales": tabp[1],
        "w1": (n((K, R)) * 1 / np.sqrt(K) * fk[:, None]).astype(np.float32),
        "floor": (np.random.uniform(0.2, 0.8, (R, 1))).astype(np.float32),
        "rs": (np.random.uniform(0.5, 2.0, (R, 1)) * fr[:, None]).astype(np.float32),
        "wor": (n((R, F)) * 1 / np.sqrt(R) / fr[:, None]).astype(np.float32),
        "res": (n((F, M)) * 0.5).astype(np.float32),
        "offs": striped(idx),
        "offs2": striped(idx2),
        "offs3": striped(idx3),
    }


def reference(tab_words, tab_scales, w1, floor, rs, wor, res, offs, offs2, offs3):
    idx = unstriped(offs)
    idx2 = unstriped(offs2)
    idx3 = unstriped(offs3)
    tabu = unpack_weight(tab_words, tab_scales, "e2m1")
    w1q = mxq(f64(w1), 0, "e4m3")
    tabidxg = tabu[:, idx]
    a = w1q.T @ tabidxg
    h0 = softplus(a)
    h1 = np.log(h0 + f64(floor))
    u1 = (h1[:, idx2] - h1[:, idx3]) * sigmoid(h1[:, idx2])
    fo1 = u1 * f64(rs)
    worq = mxq(f64(wor), 0, "e4m3")
    fo1q = mxq(fo1, 0, "e4m3")
    yo = worq.T @ fo1q
    y = yo + f64(res)
    words, scales = planes(y)
    return y, words, scales

@@ -1,0 +1,200 @@
+from contextlib import ExitStack
+
+import concourse.mybir as mybir
+
+K, R, F, T, J, M = 512, 512, 512, 2048, 512, 256
+FLOPS = 2 * K * R * J + 2 * R * F * M
+
+F32 = mybir.dt.float32
+BF16 = mybir.dt.bfloat16
+I32 = mybir.dt.int32
+U32 = mybir.dt.uint32
+U16 = mybir.dt.uint16
+U8 = mybir.dt.uint8
+FP8X4 = mybir.dt.float8_e4m3fn_x4
+FP4X4 = mybir.dt.float4_e2m1fn_x4
+ALU = mybir.AluOpType
+ACT = mybir.ActivationFunctionType
+
+P = 128
+PACK = 4
+JH = J // 2
+MH = M // 2
+LN_GUARD = 2.0 ** -57
+W1_SCALAR_COLS = 44
+
+
+def dealt_views(grouped, raw, m0, m1):
+    dst = grouped[:].rearrange("p t m j -> p m t j")[:, m0:m1]
+    src = raw[:].rearrange("p j (m t) -> p m t j", t=PACK)[:, m0:m1]
+    return dst, src
+
+
+def woven_views(grouped, planes):
+    dst = grouped.rearrange("p (c i) t -> p c t i", i=4)
+    src = planes.rearrange("p t (c i) -> p c t i", i=4)
+    return dst, src
+
+
+def tile_attend_chlogratios_pl_kernel(
+    tc, tab_words, tab_scales, w1, floor, rs, wor, res, offs, offs2, offs3, out_0, out_1, out_2
+):
+    nc = tc.nc
+    with ExitStack() as ctx:
+        lists = ctx.enter_context(tc.tile_pool(name="lists", bufs=1))
+        sb = ctx.enter_context(tc.tile_pool(name="sb", bufs=1))
+        psum = ctx.enter_context(tc.psum_pool(name="psum", bufs=1))
+
+        idx = lists.tile([P, J // 16], U16, name="idx")
+        idx2 = lists.tile([P, M // 16], U16, name="idx2")
+        idx3 = lists.tile([P, M // 16], U16, name="idx3")
+
+        tab_s = sb.tile([P, T], U8, name="tab_s", tag="scales_w1bf_floor", align_bytes=64)
+        tab_w = sb.tile([P, T], U16, name="tab_w", tag="words_then_res", align_bytes=64)
+        w1_raw = sb.tile([P, PACK, R], F32, name="w1_raw", tag="raw_weights", align_bytes=64)
+
+        nc.vector.memset(tab_s[:].bitcast(I32), 0)
+        warm_in = sb.tile([P, 1], F32, name="warm_in", align_bytes=64)
+        warm_out = sb.tile([P, 1], F32, name="warm_out", align_bytes=64)
+        nc.vector.memset(warm_in[:], 0.0)
+
+        nc.sync.dma_start(idx[:], offs)
+        for q in range(4):
+            nc.scalar.dma_start(
+                tab_s[32 * q : 32 * q + 4, :].bitcast(I32),
+                tab_scales[0, 4 * q : 4 * q + 4, :].bitcast(I32),
+            )
+        nc.sync.dma_start(tab_w[:].bitcast(I32), tab_words[0].bitcast(I32))
+        nc.sync.dma_start(w1_raw[:], w1.rearrange("(p j) r -> p j r", j=PACK))
+        nc.sync.dma_start(idx2[:], offs2)
+        nc.sync.dma_start(idx3[:], offs3)
+        nc.scalar.activation(warm_out[:], warm_in[:], ACT.Sigmoid)
+
+        g_w = sb.tile([P, J], U16, name="g_w", tag="gathered_words_then_rs", align_bytes=64)
+        nc.vector.tensor_copy(g_w[:], tab_w[:].indirect(idx[:]))
+        res_sb = sb.tile([P, PACK, M], F32, name="res_sb", tag="words_then_res", align_bytes=64)
+        g_s = sb.tile([P, J], U8, name="g_s", align_bytes=64)
+        nc.vector.tensor_copy(g_s[:], tab_s[:].indirect(idx[:]))
+
+        w1_bf = sb.tile([P, PACK, P, PACK], BF16, name="w1_bf", tag="scales_w1bf_floor", align_bytes=64)
+        dst, src = dealt_views(w1_bf, w1_raw, 0, W1_SCALAR_COLS)
+        nc.scalar.copy(dst, src)
+        dst, src = dealt_views(w1_bf, w1_raw, W1_SCALAR_COLS, P)
+        nc.vector.tensor_copy(dst, src)
+        wor_raw = sb.tile([P, PACK, F], F32, name="wor_raw", tag="raw_weights", align_bytes=64)
+        nc.sync.dma_start(wor_raw[:], wor.rearrange("(p j) f -> p j f", j=PACK))
+        w1_c = sb.tile([P, R], U32, name="w1_c", align_bytes=64)
+        w1_s = sb.tile([P, R], U8, name="w1_s", align_bytes=64)
+        a = [psum.tile([P, J], F32, name="a%d" % t) for t in range(PACK)]
+        sig_a = [sb.tile([P, J], F32, name="sig_a%d" % t, align_bytes=64) for t in range(PACK)]
+        for t in range(PACK):
+            cols = slice(t * P, (t + 1) * P)
+            nc.vector.quantize_mx(
+                out=w1_c[:, cols].bitcast(FP8X4), scales=w1_s[:, cols], in_=w1_bf[:, t].rearrange("p m j -> p (m j)")
+            )
+            nc.tensor.matmul_mx(
+                out=a[t][:],
+                lhsT=w1_c[:, cols].bitcast(FP8X4),
+                lhsT_scale=w1_s[:, cols],
+                rhs=g_w[:].bitcast(FP4X4),
+                rhs_scale=g_s[:],
+                start=True,
+                stop=True,
+            )
+            nc.scalar.activation(sig_a[t][:], a[t][:], ACT.Sigmoid, scale=-1.0)
+        floor_sb = sb.tile([P, PACK], F32, name="floor_sb", tag="scales_w1bf_floor", align_bytes=64)
+        nc.sync.dma_start(floor_sb[:], floor.rearrange("(p t) o -> p (t o)", t=PACK))
+        rs_sb = sb.tile([P, PACK], F32, name="rs_sb", tag="gathered_words_then_rs", align_bytes=64)
+        nc.sync.dma_start(rs_sb[:], rs.rearrange("(p t) o -> p (t o)", t=PACK))
+        nc.sync.dma_start(res_sb[:], res.rearrange("(p t) m -> p t m", t=PACK))
+
+        neg_rs = sb.tile([P, PACK], F32, name="neg_rs", align_bytes=64)
+        nc.vector.tensor_scalar_mul(neg_rs[:], rs_sb[:], -1.0)
+        wor_bf = sb.tile([P, PACK, P, PACK], BF16, name="wor_bf", align_bytes=64)
+        dst, src = dealt_views(wor_bf, wor_raw, 0, P)
+        nc.vector.tensor_copy(dst, src)
+        wor_c = sb.tile([P, F], U32, name="wor_c", align_bytes=64)
+        wor_s = sb.tile([P, F], U8, name="wor_s", align_bytes=64)
+        nc.vector.quantize_mx(
+            out=wor_c[:].bitcast(FP8X4), scales=wor_s[:], in_=wor_bf[:].rearrange("p t m j -> p (t m j)")
+        )
+
+        ln_sig = [sb.tile([P, J], F32, name="ln_sig%d" % t, align_bytes=64) for t in range(PACK)]
+        neg_h0 = sb.tile([P, PACK * J], F32, name="neg_h0", align_bytes=64)
+        h1 = [sb.tile([P, J], F32, name="h1_%d" % t, align_bytes=64) for t in range(PACK)]
+        for t in range(PACK):
+            nc.scalar.activation(ln_sig[t][:], sig_a[t][:], ACT.Ln, bias=LN_GUARD)
+        for t in range(PACK):
+            nc.vector.scalar_tensor_tensor(
+                neg_h0[:, t * J : (t + 1) * J], a[t][:], -1.0, ln_sig[t][:], ALU.mult, ALU.min
+            )
+        for t in range(PACK):
+            nc.scalar.activation(
+                h1[t][:], neg_h0[:, t * J : (t + 1) * J], ACT.Ln, bias=floor_sb[:, t : t + 1], scale=-1.0
+            )
+
+        first = sb.tile([P, PACK * M], F32, name="first", align_bytes=64)
+        neg_diff = sb.tile([P, PACK * M], F32, name="neg_diff", align_bytes=64)
+        for t in range(PACK):
+            cols = slice(t * M, (t + 1) * M)
+            nc.vector.tensor_copy(first[:, cols], h1[t][:].indirect(idx2[:]))
+        for t in range(PACK):
+            cols = slice(t * M, (t + 1) * M)
+            nc.vector.tensor_tensor(neg_diff[:, cols], h1[t][:].indirect(idx3[:]), first[:, cols], ALU.subtract)
+
+        gate = sb.tile([P, PACK * M], F32, name="gate", align_bytes=64)
+        nc.scalar.activation(gate[:], first[:], ACT.Sigmoid)
+        fo1 = sb.tile([P, PACK, M], F32, name="fo1", align_bytes=64)
+        for t in range(PACK):
+            cols = slice(t * M, (t + 1) * M)
+            nc.vector.scalar_tensor_tensor(
+                fo1[:, t, :], neg_diff[:, cols], neg_rs[:, t : t + 1], gate[:, cols], ALU.mult, ALU.mult
+            )
+
+        fo1_bf = [sb.tile([P, MH, PACK], BF16, name="fo1_bf%d" % h, align_bytes=64) for h in range(2)]
+        fo1_c = [sb.tile([P, MH], U32, name="fo1_c%d" % h, align_bytes=64) for h in range(2)]
+        fo1_s = [sb.tile([P, MH], U8, name="fo1_s%d" % h, align_bytes=64) for h in range(2)]
+        yo = [psum.tile([P, PACK, MH], F32, name="yo%d" % h) for h in range(2)]
+        y = [sb.tile([P, PACK, MH], F32, name="y%d" % h, align_bytes=64) for h in range(2)]
+        y_bf = [sb.tile([P, MH, PACK], BF16, name="y_bf%d" % h, align_bytes=64) for h in range(2)]
+        y_c = sb.tile([P, M], U32, name="y_c", align_bytes=64)
+        y_s = sb.tile([P, M], U8, name="y_s", align_bytes=64)
+        out_rows = out_0.rearrange("(p t) m -> p t m", t=PACK)
+
+        dst, src = woven_views(fo1_bf[0][:], fo1[:, :, 0:MH])
+        nc.vector.tensor_copy(dst, src)
+        dst, src = woven_views(fo1_bf[1][:], fo1[:, :, MH:M])
+        nc.scalar.copy(dst, src)
+        for h in range(2):
+            nc.vector.quantize_mx(
+                out=fo1_c[h][:].bitcast(FP8X4), scales=fo1_s[h][:], in_=fo1_bf[h][:].rearrange("p m t -> p (m t)")
+            )
+            for t in range(PACK):
+                nc.tensor.matmul_mx(
+                    out=yo[h][:, t, :],
+                    lhsT=wor_c[:, t * P : (t + 1) * P].bitcast(FP8X4),
+                    lhsT_scale=wor_s[:, t * P : (t + 1) * P],
+                    rhs=fo1_c[h][:].bitcast(FP8X4),
+                    rhs_scale=fo1_s[h][:],
+                    start=True,
+                    stop=True,
+                )
+        for h in range(2):
+            cols = slice(h * MH, (h + 1) * MH)
+            nc.vector.tensor_tensor(y[h][:], yo[h][:], res_sb[:, :, cols], ALU.add)
+            nc.sync.dma_start(out_rows[:, :, cols], y[h][:])
+        dst, src = woven_views(y_bf[0][:], y[0][:])
+        nc.scalar.copy(dst, src)
+        dst, src = woven_views(y_bf[1][:], y[1][:])
+        nc.vector.tensor_copy(dst, src)
+        for h in range(2):
+            cols = slice(h * MH, (h + 1) * MH)
+            nc.vector.quantize_mx(
+                out=y_c[:, cols].bitcast(FP8X4), scales=y_s[:, cols], in_=y_bf[h][:].rearrange("p m t -> p (m t)")
+            )
+        nc.sync.dma_start(out_1[0].rearrange("p c r -> p (c r)").bitcast(I32), y_c[:].bitcast(I32))
+        for q in range(4):
+            queue = nc.scalar if q % 2 else nc.sync
+            queue.dma_start(
+                out_2[0, 4 * q : 4 * q + 4, :].bitcast(I32), y_s[32 * q : 32 * q + 4, :].bitcast(I32)
+            )

@@ -20,8 +20,9 @@ P = 128
 PACK = 4
 JH = J // 2
 MH = M // 2
-LN_GUARD = 2.0 ** -57
+SATURATION = 40.0
 W1_SCALAR_COLS = 44
+VECTOR_SCALED = 2
 
 
 def dealt_views(grouped, raw, m0, m1):
@@ -49,40 +50,46 @@ def tile_attend_chlogratios_pl_kernel(
         idx2 = lists.tile([P, M // 16], U16, name="idx2")
         idx3 = lists.tile([P, M // 16], U16, name="idx3")
 
-        tab_s = sb.tile([P, T], U8, name="tab_s", tag="scales_w1bf_floor", align_bytes=64)
-        tab_w = sb.tile([P, T], U16, name="tab_w", tag="words_then_res", align_bytes=64)
-        w1_raw = sb.tile([P, PACK, R], F32, name="w1_raw", tag="raw_weights", align_bytes=64)
+        tab_s = sb.tile([P, T], U8, name="tab_s", align_bytes=64)
+        tab_w = sb.tile([P, T], U16, name="tab_w", align_bytes=64)
+        w1_raw = sb.tile([P, PACK, R], F32, name="w1_raw", align_bytes=64)
 
-        nc.vector.memset(tab_s[:].bitcast(I32), 0)
-        warm_in = sb.tile([P, 1], F32, name="warm_in", align_bytes=64)
-        warm_out = sb.tile([P, 1], F32, name="warm_out", align_bytes=64)
-        nc.vector.memset(warm_in[:], 0.0)
+        wor_raw = sb.tile([P, PACK, F], F32, name="wor_raw", align_bytes=64)
+        res_sb = sb.tile([P, PACK, M], F32, name="res_sb", align_bytes=64)
+        floor_sb = sb.tile([P, PACK], F32, name="floor_sb", align_bytes=64)
+        rs_sb = sb.tile([P, PACK], F32, name="rs_sb", align_bytes=64)
+        nc.vector.memset(tab_s[:, 0 : T // 2].bitcast(I32), 0)
+        nc.gpsimd.memset(tab_s[:, T // 2 : T].bitcast(I32), 0)
+        neg_sat = sb.tile([P, 1], F32, name="neg_sat", align_bytes=64)
+        ln_guard = sb.tile([P, 1], F32, name="ln_guard", align_bytes=64)
+        nc.vector.memset(neg_sat[:], -SATURATION)
 
         nc.sync.dma_start(idx[:], offs)
+        nc.sync.dma_start(tab_w[:].bitcast(I32), tab_words[0].bitcast(I32))
+        nc.sync.dma_start(idx2[:], offs2)
         for q in range(4):
-            nc.scalar.dma_start(
+            nc.sync.dma_start(
                 tab_s[32 * q : 32 * q + 4, :].bitcast(I32),
                 tab_scales[0, 4 * q : 4 * q + 4, :].bitcast(I32),
             )
-        nc.sync.dma_start(tab_w[:].bitcast(I32), tab_words[0].bitcast(I32))
         nc.sync.dma_start(w1_raw[:], w1.rearrange("(p j) r -> p j r", j=PACK))
-        nc.sync.dma_start(idx2[:], offs2)
         nc.sync.dma_start(idx3[:], offs3)
-        nc.scalar.activation(warm_out[:], warm_in[:], ACT.Sigmoid)
+        nc.sync.dma_start(wor_raw[:], wor.rearrange("(p j) f -> p j f", j=PACK))
+        nc.sync.dma_start(floor_sb[:], floor.rearrange("(p t) o -> p (t o)", t=PACK))
+        nc.sync.dma_start(rs_sb[:], rs.rearrange("(p t) o -> p (t o)", t=PACK))
+        nc.sync.dma_start(res_sb[:], res.rearrange("(p t) m -> p t m", t=PACK))
+        nc.scalar.activation(ln_guard[:], neg_sat[:], ACT.Sigmoid)
 
-        g_w = sb.tile([P, J], U16, name="g_w", tag="gathered_words_then_rs", align_bytes=64)
+        g_w = sb.tile([P, J], U16, name="g_w", align_bytes=64)
         nc.vector.tensor_copy(g_w[:], tab_w[:].indirect(idx[:]))
-        res_sb = sb.tile([P, PACK, M], F32, name="res_sb", tag="words_then_res", align_bytes=64)
         g_s = sb.tile([P, J], U8, name="g_s", align_bytes=64)
         nc.vector.tensor_copy(g_s[:], tab_s[:].indirect(idx[:]))
 
-        w1_bf = sb.tile([P, PACK, P, PACK], BF16, name="w1_bf", tag="scales_w1bf_floor", align_bytes=64)
+        w1_bf = sb.tile([P, PACK, P, PACK], BF16, name="w1_bf", align_bytes=64)
         dst, src = dealt_views(w1_bf, w1_raw, 0, W1_SCALAR_COLS)
         nc.scalar.copy(dst, src)
         dst, src = dealt_views(w1_bf, w1_raw, W1_SCALAR_COLS, P)
         nc.vector.tensor_copy(dst, src)
-        wor_raw = sb.tile([P, PACK, F], F32, name="wor_raw", tag="raw_weights", align_bytes=64)
-        nc.sync.dma_start(wor_raw[:], wor.rearrange("(p j) f -> p j f", j=PACK))
         w1_c = sb.tile([P, R], U32, name="w1_c", align_bytes=64)
         w1_s = sb.tile([P, R], U8, name="w1_s", align_bytes=64)
         a = [psum.tile([P, J], F32, name="a%d" % t) for t in range(PACK)]
@@ -102,11 +109,6 @@ def tile_attend_chlogratios_pl_kernel(
                 stop=True,
             )
             nc.scalar.activation(sig_a[t][:], a[t][:], ACT.Sigmoid, scale=-1.0)
-        floor_sb = sb.tile([P, PACK], F32, name="floor_sb", tag="scales_w1bf_floor", align_bytes=64)
-        nc.sync.dma_start(floor_sb[:], floor.rearrange("(p t) o -> p (t o)", t=PACK))
-        rs_sb = sb.tile([P, PACK], F32, name="rs_sb", tag="gathered_words_then_rs", align_bytes=64)
-        nc.sync.dma_start(rs_sb[:], rs.rearrange("(p t) o -> p (t o)", t=PACK))
-        nc.sync.dma_start(res_sb[:], res.rearrange("(p t) m -> p t m", t=PACK))
 
         neg_rs = sb.tile([P, PACK], F32, name="neg_rs", align_bytes=64)
         nc.vector.tensor_scalar_mul(neg_rs[:], rs_sb[:], -1.0)
@@ -123,7 +125,7 @@ def tile_attend_chlogratios_pl_kernel(
         neg_h0 = sb.tile([P, PACK * J], F32, name="neg_h0", align_bytes=64)
         h1 = [sb.tile([P, J], F32, name="h1_%d" % t, align_bytes=64) for t in range(PACK)]
         for t in range(PACK):
-            nc.scalar.activation(ln_sig[t][:], sig_a[t][:], ACT.Ln, bias=LN_GUARD)
+            nc.scalar.activation(ln_sig[t][:], sig_a[t][:], ACT.Ln, bias=ln_guard[:])
         for t in range(PACK):
             nc.vector.scalar_tensor_tensor(
                 neg_h0[:, t * J : (t + 1) * J], a[t][:], -1.0, ln_sig[t][:], ALU.mult, ALU.min
@@ -140,38 +142,45 @@ def tile_attend_chlogratios_pl_kernel(
             nc.vector.tensor_copy(first[:, cols], h1[t][:].indirect(idx2[:]))
         for t in range(PACK):
             cols = slice(t * M, (t + 1) * M)
-            nc.vector.tensor_tensor(neg_diff[:, cols], h1[t][:].indirect(idx3[:]), first[:, cols], ALU.subtract)
+            for m0, m1 in ((0, M),) if t < PACK - 1 else ((0, MH), (MH, M)):
+                cols = slice(t * M + m0, t * M + m1)
+                nc.vector.tensor_tensor(
+                    neg_diff[:, cols], h1[t][:].indirect(idx3[:, m0 // 16 : m1 // 16]), first[:, cols], ALU.subtract
+                )
 
-        gate = sb.tile([P, PACK * M], F32, name="gate", align_bytes=64)
-        nc.scalar.activation(gate[:], first[:], ACT.Sigmoid)
-        fo1 = sb.tile([P, PACK, M], F32, name="fo1", align_bytes=64)
-        for t in range(PACK):
-            cols = slice(t * M, (t + 1) * M)
-            nc.vector.scalar_tensor_tensor(
-                fo1[:, t, :], neg_diff[:, cols], neg_rs[:, t : t + 1], gate[:, cols], ALU.mult, ALU.mult
-            )
+        first_planes = first[:].rearrange("p (t m) -> p t m", t=PACK)
+        diff_planes = neg_diff[:].rearrange("p (t m) -> p t m", t=PACK)
+        gate = [neg_h0[:, (3 - h) * J : (4 - h) * J].rearrange("p (t m) -> p t m", t=PACK) for h in range(2)]
+        for h in range(2):
+            cols = slice(h * MH, (h + 1) * MH)
+            for t0, t1 in ((0, 2), (2, 4)) if h == 0 else ((0, 4),):
+                nc.scalar.activation(gate[h][:, t0:t1, :], first_planes[:, t0:t1, cols], ACT.Sigmoid)
+            for t in range(PACK) if h == 0 else range(VECTOR_SCALED, PACK):
+                nc.scalar.activation(gate[h][:, t, :], gate[h][:, t, :], ACT.Copy, scale=neg_rs[:, t : t + 1])
 
-        fo1_bf = [sb.tile([P, MH, PACK], BF16, name="fo1_bf%d" % h, align_bytes=64) for h in range(2)]
+        fo1_bf = [
+            sb.tile([P, MH, PACK], BF16, name="fo1_bf%d" % h, tag="fo1_bf%d" % h, align_bytes=64) for h in range(2)
+        ]
         fo1_c = [sb.tile([P, MH], U32, name="fo1_c%d" % h, align_bytes=64) for h in range(2)]
         fo1_s = [sb.tile([P, MH], U8, name="fo1_s%d" % h, align_bytes=64) for h in range(2)]
-        yo = [psum.tile([P, PACK, MH], F32, name="yo%d" % h) for h in range(2)]
-        y = [sb.tile([P, PACK, MH], F32, name="y%d" % h, align_bytes=64) for h in range(2)]
+        yo = [[psum.tile([P, 2, MH], F32, name="yo%d_%d" % (h, g)) for g in range(2)] for h in range(2)]
         y_bf = [sb.tile([P, MH, PACK], BF16, name="y_bf%d" % h, align_bytes=64) for h in range(2)]
         y_c = sb.tile([P, M], U32, name="y_c", align_bytes=64)
         y_s = sb.tile([P, M], U8, name="y_s", align_bytes=64)
         out_rows = out_0.rearrange("(p t) m -> p t m", t=PACK)
 
-        dst, src = woven_views(fo1_bf[0][:], fo1[:, :, 0:MH])
-        nc.vector.tensor_copy(dst, src)
-        dst, src = woven_views(fo1_bf[1][:], fo1[:, :, MH:M])
-        nc.scalar.copy(dst, src)
         for h in range(2):
+            for t in range(VECTOR_SCALED if h == 1 else 0):
+                nc.vector.tensor_scalar_mul(diff_planes[:, t, MH:M], diff_planes[:, t, MH:M], neg_rs[:, t : t + 1])
+            dst, diff_src = woven_views(fo1_bf[h][:], diff_planes[:, :, h * MH : (h + 1) * MH])
+            dst, gate_src = woven_views(fo1_bf[h][:], gate[h])
+            nc.vector.tensor_tensor(dst, diff_src, gate_src, ALU.mult)
             nc.vector.quantize_mx(
                 out=fo1_c[h][:].bitcast(FP8X4), scales=fo1_s[h][:], in_=fo1_bf[h][:].rearrange("p m t -> p (m t)")
             )
             for t in range(PACK):
                 nc.tensor.matmul_mx(
-                    out=yo[h][:, t, :],
+                    out=yo[h][t // 2][:, t % 2, :],
                     lhsT=wor_c[:, t * P : (t + 1) * P].bitcast(FP8X4),
                     lhsT_scale=wor_s[:, t * P : (t + 1) * P],
                     rhs=fo1_c[h][:].bitcast(FP8X4),
@@ -179,20 +188,29 @@ def tile_attend_chlogratios_pl_kernel(
                     start=True,
                     stop=True,
                 )
+        y = [
+            sb.tile([P, PACK, MH], F32, name="y0", tag="fo1_bf1", align_bytes=64),
+            sb.tile([P, PACK, MH], F32, name="y1", align_bytes=64),
+        ]
         for h in range(2):
             cols = slice(h * MH, (h + 1) * MH)
-            nc.vector.tensor_tensor(y[h][:], yo[h][:], res_sb[:, :, cols], ALU.add)
+            for g in range(2):
+                rows = slice(2 * g, 2 * g + 2)
+                nc.vector.tensor_tensor(y[h][:, rows, :], yo[h][g][:], res_sb[:, rows, cols], ALU.add)
             nc.sync.dma_start(out_rows[:, :, cols], y[h][:])
         dst, src = woven_views(y_bf[0][:], y[0][:])
         nc.scalar.copy(dst, src)
-        dst, src = woven_views(y_bf[1][:], y[1][:])
+        dst, src = woven_views(y_bf[1][:, 0 : MH // 2], y[1][:, :, 0 : MH // 2])
+        nc.scalar.copy(dst, src)
+        dst, src = woven_views(y_bf[1][:, MH // 2 : MH], y[1][:, :, MH // 2 : MH])
         nc.vector.tensor_copy(dst, src)
+        out_words = out_1[0].rearrange("p c r -> p (c r)").bitcast(I32)
         for h in range(2):
             cols = slice(h * MH, (h + 1) * MH)
             nc.vector.quantize_mx(
                 out=y_c[:, cols].bitcast(FP8X4), scales=y_s[:, cols], in_=y_bf[h][:].rearrange("p m t -> p (m t)")
             )
-        nc.sync.dma_start(out_1[0].rearrange("p c r -> p (c r)").bitcast(I32), y_c[:].bitcast(I32))
+            nc.sync.dma_start(out_words[:, cols], y_c[:, cols].bitcast(I32))
         for q in range(4):
             queue = nc.scalar if q % 2 else nc.sync
             queue.dma_start(

@@ -21,14 +21,12 @@ PACK = 4
 JH = J // 2
 MH = M // 2
 SATURATION = 40.0
-W1_SCALAR_COLS = 44
+W1_SCALAR_COLS = 16
 VECTOR_SCALED = 2
 
 
-def dealt_views(grouped, raw, m0, m1):
-    dst = grouped[:].rearrange("p t m j -> p m t j")[:, m0:m1]
-    src = raw[:].rearrange("p j (m t) -> p m t j", t=PACK)[:, m0:m1]
-    return dst, src
+def dealt_views(grouped, raw):
+    return grouped.rearrange("p t m j -> p m t j"), raw.rearrange("p j (m t) -> p m t j", t=PACK)
 
 
 def woven_views(grouped, planes):
@@ -52,7 +50,7 @@ def tile_attend_chlogratios_pl_kernel(
 
         tab_s = sb.tile([P, T], U8, name="tab_s", align_bytes=64)
         tab_w = sb.tile([P, T], U16, name="tab_w", align_bytes=64)
-        w1_raw = sb.tile([P, PACK, R], F32, name="w1_raw", align_bytes=64)
+        w1_raw = [sb.tile([P, PACK, R // 2], F32, name="w1_raw%d" % c, align_bytes=64) for c in range(2)]
 
         wor_raw = sb.tile([P, PACK, F], F32, name="wor_raw", align_bytes=64)
         res_sb = sb.tile([P, PACK, M], F32, name="res_sb", align_bytes=64)
@@ -72,7 +70,8 @@ def tile_attend_chlogratios_pl_kernel(
                 tab_s[32 * q : 32 * q + 4, :].bitcast(I32),
                 tab_scales[0, 4 * q : 4 * q + 4, :].bitcast(I32),
             )
-        nc.sync.dma_start(w1_raw[:], w1.rearrange("(p j) r -> p j r", j=PACK))
+        for c in range(2):
+            nc.sync.dma_start(w1_raw[c][:], w1.rearrange("(p j) r -> p j r", j=PACK)[:, :, c * R // 2 : (c + 1) * R // 2])
         nc.sync.dma_start(idx3[:], offs3)
         nc.sync.dma_start(wor_raw[:], wor.rearrange("(p j) f -> p j f", j=PACK))
         nc.sync.dma_start(floor_sb[:], floor.rearrange("(p t) o -> p (t o)", t=PACK))
@@ -86,10 +85,12 @@ def tile_attend_chlogratios_pl_kernel(
         nc.vector.tensor_copy(g_s[:], tab_s[:].indirect(idx[:]))
 
         w1_bf = sb.tile([P, PACK, P, PACK], BF16, name="w1_bf", align_bytes=64)
-        dst, src = dealt_views(w1_bf, w1_raw, 0, W1_SCALAR_COLS)
+        dst, src = dealt_views(w1_bf[:, :, 0 : P // 2], w1_raw[0][:])
         nc.scalar.copy(dst, src)
-        dst, src = dealt_views(w1_bf, w1_raw, W1_SCALAR_COLS, P)
-        nc.vector.tensor_copy(dst, src)
+        dst, src = dealt_views(w1_bf[:, :, P // 2 : P], w1_raw[1][:])
+        nc.scalar.copy(dst[:, 0:W1_SCALAR_COLS], src[:, 0:W1_SCALAR_COLS])
+        for t0 in (0, 2):
+            nc.vector.tensor_copy(dst[:, W1_SCALAR_COLS:, t0 : t0 + 2], src[:, W1_SCALAR_COLS:, t0 : t0 + 2])
         w1_c = sb.tile([P, R], U32, name="w1_c", align_bytes=64)
         w1_s = sb.tile([P, R], U8, name="w1_s", align_bytes=64)
         a = [psum.tile([P, J], F32, name="a%d" % t) for t in range(PACK)]
@@ -113,7 +114,7 @@ def tile_attend_chlogratios_pl_kernel(
         neg_rs = sb.tile([P, PACK], F32, name="neg_rs", align_bytes=64)
         nc.vector.tensor_scalar_mul(neg_rs[:], rs_sb[:], -1.0)
         wor_bf = sb.tile([P, PACK, P, PACK], BF16, name="wor_bf", align_bytes=64)
-        dst, src = dealt_views(wor_bf, wor_raw, 0, P)
+        dst, src = dealt_views(wor_bf[:], wor_raw[:])
         nc.vector.tensor_copy(dst, src)
         wor_c = sb.tile([P, F], U32, name="wor_c", align_bytes=64)
         wor_s = sb.tile([P, F], U8, name="wor_s", align_bytes=64)

from contextlib import ExitStack

import concourse.mybir as mybir

K, R, F, T, J, M = 512, 512, 512, 2048, 512, 256
FLOPS = 2 * K * R * J + 2 * R * F * M

F32 = mybir.dt.float32
BF16 = mybir.dt.bfloat16
I32 = mybir.dt.int32
U32 = mybir.dt.uint32
U16 = mybir.dt.uint16
U8 = mybir.dt.uint8
FP8X4 = mybir.dt.float8_e4m3fn_x4
FP4X4 = mybir.dt.float4_e2m1fn_x4
ALU = mybir.AluOpType
ACT = mybir.ActivationFunctionType

P = 128
PACK = 4
JH = J // 2
MH = M // 2
SATURATION = 40.0
W1_SCALAR_COLS = 16
VECTOR_SCALED = 2


def dealt_views(grouped, raw):
    return grouped.rearrange("p t m j -> p m t j"), raw.rearrange("p j (m t) -> p m t j", t=PACK)


def woven_views(grouped, planes):
    dst = grouped.rearrange("p (c i) t -> p c t i", i=4)
    src = planes.rearrange("p t (c i) -> p c t i", i=4)
    return dst, src


def tile_attend_chlogratios_pl_kernel(
    tc, tab_words, tab_scales, w1, floor, rs, wor, res, offs, offs2, offs3, out_0, out_1, out_2
):
    nc = tc.nc
    with ExitStack() as ctx:
        lists = ctx.enter_context(tc.tile_pool(name="lists", bufs=1))
        sb = ctx.enter_context(tc.tile_pool(name="sb", bufs=1))
        psum = ctx.enter_context(tc.psum_pool(name="psum", bufs=1))

        idx = lists.tile([P, J // 16], U16, name="idx")
        idx2 = lists.tile([P, M // 16], U16, name="idx2")
        idx3 = lists.tile([P, M // 16], U16, name="idx3")

        tab_s = sb.tile([P, T], U8, name="tab_s", align_bytes=64)
        tab_w = sb.tile([P, T], U16, name="tab_w", align_bytes=64)
        w1_raw = [sb.tile([P, PACK, R // 2], F32, name="w1_raw%d" % c, align_bytes=64) for c in range(2)]

        wor_raw = sb.tile([P, PACK, F], F32, name="wor_raw", align_bytes=64)
        res_sb = sb.tile([P, PACK, M], F32, name="res_sb", align_bytes=64)
        floor_sb = sb.tile([P, PACK], F32, name="floor_sb", align_bytes=64)
        rs_sb = sb.tile([P, PACK], F32, name="rs_sb", align_bytes=64)
        nc.vector.memset(tab_s[:, 0 : T // 2].bitcast(I32), 0)
        nc.gpsimd.memset(tab_s[:, T // 2 : T].bitcast(I32), 0)
        neg_sat = sb.tile([P, 1], F32, name="neg_sat", align_bytes=64)
        ln_guard = sb.tile([P, 1], F32, name="ln_guard", align_bytes=64)
        nc.vector.memset(neg_sat[:], -SATURATION)

        nc.sync.dma_start(idx[:], offs)
        nc.sync.dma_start(tab_w[:].bitcast(I32), tab_words[0].bitcast(I32))
        nc.sync.dma_start(idx2[:], offs2)
        for q in range(4):
            nc.sync.dma_start(
                tab_s[32 * q : 32 * q + 4, :].bitcast(I32),
                tab_scales[0, 4 * q : 4 * q + 4, :].bitcast(I32),
            )
        for c in range(2):
            nc.sync.dma_start(w1_raw[c][:], w1.rearrange("(p j) r -> p j r", j=PACK)[:, :, c * R // 2 : (c + 1) * R // 2])
        nc.sync.dma_start(idx3[:], offs3)
        nc.sync.dma_start(wor_raw[:], wor.rearrange("(p j) f -> p j f", j=PACK))
        nc.sync.dma_start(floor_sb[:], floor.rearrange("(p t) o -> p (t o)", t=PACK))
        nc.sync.dma_start(rs_sb[:], rs.rearrange("(p t) o -> p (t o)", t=PACK))
        nc.sync.dma_start(res_sb[:], res.rearrange("(p t) m -> p t m", t=PACK))
        nc.scalar.activation(ln_guard[:], neg_sat[:], ACT.Sigmoid)

        g_w = sb.tile([P, J], U16, name="g_w", align_bytes=64)
        nc.vector.tensor_copy(g_w[:], tab_w[:].indirect(idx[:]))
        g_s = sb.tile([P, J], U8, name="g_s", align_bytes=64)
        nc.vector.tensor_copy(g_s[:], tab_s[:].indirect(idx[:]))

        w1_bf = sb.tile([P, PACK, P, PACK], BF16, name="w1_bf", align_bytes=64)
        dst, src = dealt_views(w1_bf[:, :, 0 : P // 2], w1_raw[0][:])
        nc.scalar.copy(dst, src)
        dst, src = dealt_views(w1_bf[:, :, P // 2 : P], w1_raw[1][:])
        nc.scalar.copy(dst[:, 0:W1_SCALAR_COLS], src[:, 0:W1_SCALAR_COLS])
        for t0 in (0, 2):
            nc.vector.tensor_copy(dst[:, W1_SCALAR_COLS:, t0 : t0 + 2], src[:, W1_SCALAR_COLS:, t0 : t0 + 2])
        w1_c = sb.tile([P, R], U32, name="w1_c", align_bytes=64)
        w1_s = sb.tile([P, R], U8, name="w1_s", align_bytes=64)
        a = [psum.tile([P, J], F32, name="a%d" % t) for t in range(PACK)]
        sig_a = [sb.tile([P, J], F32, name="sig_a%d" % t, align_bytes=64) for t in range(PACK)]
        for t in range(PACK):
            cols = slice(t * P, (t + 1) * P)
            nc.vector.quantize_mx(
                out=w1_c[:, cols].bitcast(FP8X4), scales=w1_s[:, cols], in_=w1_bf[:, t].rearrange("p m j -> p (m j)")
            )
            nc.tensor.matmul_mx(
                out=a[t][:],
                lhsT=w1_c[:, cols].bitcast(FP8X4),
                lhsT_scale=w1_s[:, cols],
                rhs=g_w[:].bitcast(FP4X4),
                rhs_scale=g_s[:],
                start=True,
                stop=True,
            )
            nc.scalar.activation(sig_a[t][:], a[t][:], ACT.Sigmoid, scale=-1.0)

        neg_rs = sb.tile([P, PACK], F32, name="neg_rs", align_bytes=64)
        nc.vector.tensor_scalar_mul(neg_rs[:], rs_sb[:], -1.0)
        wor_bf = sb.tile([P, PACK, P, PACK], BF16, name="wor_bf", align_bytes=64)
        dst, src = dealt_views(wor_bf[:], wor_raw[:])
        nc.vector.tensor_copy(dst, src)
        wor_c = sb.tile([P, F], U32, name="wor_c", align_bytes=64)
        wor_s = sb.tile([P, F], U8, name="wor_s", align_bytes=64)
        nc.vector.quantize_mx(
            out=wor_c[:].bitcast(FP8X4), scales=wor_s[:], in_=wor_bf[:].rearrange("p t m j -> p (t m j)")
        )

        ln_sig = [sb.tile([P, J], F32, name="ln_sig%d" % t, align_bytes=64) for t in range(PACK)]
        neg_h0 = sb.tile([P, PACK * J], F32, name="neg_h0", align_bytes=64)
        h1 = [sb.tile([P, J], F32, name="h1_%d" % t, align_bytes=64) for t in range(PACK)]
        for t in range(PACK):
            nc.scalar.activation(ln_sig[t][:], sig_a[t][:], ACT.Ln, bias=ln_guard[:])
        for t in range(PACK):
            nc.vector.scalar_tensor_tensor(
                neg_h0[:, t * J : (t + 1) * J], a[t][:], -1.0, ln_sig[t][:], ALU.mult, ALU.min
            )
        for t in range(PACK):
            nc.scalar.activation(
                h1[t][:], neg_h0[:, t * J : (t + 1) * J], ACT.Ln, bias=floor_sb[:, t : t + 1], scale=-1.0
            )

        first = sb.tile([P, PACK * M], F32, name="first", align_bytes=64)
        neg_diff = sb.tile([P, PACK * M], F32, name="neg_diff", align_bytes=64)
        for t in range(PACK):
            cols = slice(t * M, (t + 1) * M)
            nc.vector.tensor_copy(first[:, cols], h1[t][:].indirect(idx2[:]))
        for t in range(PACK):
            cols = slice(t * M, (t + 1) * M)
            for m0, m1 in ((0, M),) if t < PACK - 1 else ((0, MH), (MH, M)):
                cols = slice(t * M + m0, t * M + m1)
                nc.vector.tensor_tensor(
                    neg_diff[:, cols], h1[t][:].indirect(idx3[:, m0 // 16 : m1 // 16]), first[:, cols], ALU.subtract
                )

        first_planes = first[:].rearrange("p (t m) -> p t m", t=PACK)
        diff_planes = neg_diff[:].rearrange("p (t m) -> p t m", t=PACK)
        gate = [neg_h0[:, (3 - h) * J : (4 - h) * J].rearrange("p (t m) -> p t m", t=PACK) for h in range(2)]
        for h in range(2):
            cols = slice(h * MH, (h + 1) * MH)
            for t0, t1 in ((0, 2), (2, 4)) if h == 0 else ((0, 4),):
                nc.scalar.activation(gate[h][:, t0:t1, :], first_planes[:, t0:t1, cols], ACT.Sigmoid)
            for t in range(PACK) if h == 0 else range(VECTOR_SCALED, PACK):
                nc.scalar.activation(gate[h][:, t, :], gate[h][:, t, :], ACT.Copy, scale=neg_rs[:, t : t + 1])

        fo1_bf = [
            sb.tile([P, MH, PACK], BF16, name="fo1_bf%d" % h, tag="fo1_bf%d" % h, align_bytes=64) for h in range(2)
        ]
        fo1_c = [sb.tile([P, MH], U32, name="fo1_c%d" % h, align_bytes=64) for h in range(2)]
        fo1_s = [sb.tile([P, MH], U8, name="fo1_s%d" % h, align_bytes=64) for h in range(2)]
        yo = [[psum.tile([P, 2, MH], F32, name="yo%d_%d" % (h, g)) for g in range(2)] for h in range(2)]
        y_bf = [sb.tile([P, MH, PACK], BF16, name="y_bf%d" % h, align_bytes=64) for h in range(2)]
        y_c = sb.tile([P, M], U32, name="y_c", align_bytes=64)
        y_s = sb.tile([P, M], U8, name="y_s", align_bytes=64)
        out_rows = out_0.rearrange("(p t) m -> p t m", t=PACK)

        for h in range(2):
            for t in range(VECTOR_SCALED if h == 1 else 0):
                nc.vector.tensor_scalar_mul(diff_planes[:, t, MH:M], diff_planes[:, t, MH:M], neg_rs[:, t : t + 1])
            dst, diff_src = woven_views(fo1_bf[h][:], diff_planes[:, :, h * MH : (h + 1) * MH])
            dst, gate_src = woven_views(fo1_bf[h][:], gate[h])
            nc.vector.tensor_tensor(dst, diff_src, gate_src, ALU.mult)
            nc.vector.quantize_mx(
                out=fo1_c[h][:].bitcast(FP8X4), scales=fo1_s[h][:], in_=fo1_bf[h][:].rearrange("p m t -> p (m t)")
            )
            for t in range(PACK):
                nc.tensor.matmul_mx(
                    out=yo[h][t // 2][:, t % 2, :],
                    lhsT=wor_c[:, t * P : (t + 1) * P].bitcast(FP8X4),
                    lhsT_scale=wor_s[:, t * P : (t + 1) * P],
                    rhs=fo1_c[h][:].bitcast(FP8X4),
                    rhs_scale=fo1_s[h][:],
                    start=True,
                    stop=True,
                )
        y = [
            sb.tile([P, PACK, MH], F32, name="y0", tag="fo1_bf1", align_bytes=64),
            sb.tile([P, PACK, MH], F32, name="y1", align_bytes=64),
        ]
        for h in range(2):
            cols = slice(h * MH, (h + 1) * MH)
            for g in range(2):
                rows = slice(2 * g, 2 * g + 2)
                nc.vector.tensor_tensor(y[h][:, rows, :], yo[h][g][:], res_sb[:, rows, cols], ALU.add)
            nc.sync.dma_start(out_rows[:, :, cols], y[h][:])
        dst, src = woven_views(y_bf[0][:], y[0][:])
        nc.scalar.copy(dst, src)
        dst, src = woven_views(y_bf[1][:, 0 : MH // 2], y[1][:, :, 0 : MH // 2])
        nc.scalar.copy(dst, src)
        dst, src = woven_views(y_bf[1][:, MH // 2 : MH], y[1][:, :, MH // 2 : MH])
        nc.vector.tensor_copy(dst, src)
        out_words = out_1[0].rearrange("p c r -> p (c r)").bitcast(I32)
        for h in range(2):
            cols = slice(h * MH, (h + 1) * MH)
            nc.vector.quantize_mx(
                out=y_c[:, cols].bitcast(FP8X4), scales=y_s[:, cols], in_=y_bf[h][:].rearrange("p m t -> p (m t)")
            )
            nc.sync.dma_start(out_words[:, cols], y_c[:, cols].bitcast(I32))
        for q in range(4):
            queue = nc.scalar if q % 2 else nc.sync
            queue.dma_start(
                out_2[0, 4 * q : 4 * q + 4, :].bitcast(I32), y_s[32 * q : 32 * q + 4, :].bitcast(I32)
            )
